import numpy as np
import ml_dtypes


def mxq(x, axis, fmt="e4m3"):
    dtype, down = {"e4m3": (ml_dtypes.float8_e4m3fn, 7), "e5m2": (ml_dtypes.float8_e5m2, 14)}[fmt]
    v = np.moveaxis(np.asarray(x, np.float32).astype(ml_dtypes.bfloat16).astype(np.float64), axis, -1)
    blocks = v.reshape(v.shape[:-1] + (-1, 32))
    amax = np.abs(blocks).max(-1, keepdims=True)
    byte = np.maximum(np.where(amax > 0, np.frexp(amax)[1] - 1 + 127, 0) - down, 1)
    scale = np.exp2(byte - 127.0)
    codes = (blocks / scale).astype(np.float32).astype(dtype).astype(np.float64)
    return np.moveaxis((codes * scale).reshape(v.shape), -1, axis)


WIDE = False


def mx_kscale(k):
    if not WIDE:
        return np.ones(k)
    levels = np.array([10, -10, 5, -5, 0])
    if k % 512:
        return np.exp2(np.random.permutation(np.resize(levels, k // 32))).repeat(32)
    a = np.empty((k // 512, 16))
    for p in range(k // 512):
        a[p, :8] = np.random.permutation(np.resize(levels, 8))
        for g in range(8):
            far = levels[np.abs(levels - a[p, g]) >= 10]
            a[p, g + 8] = far[np.random.randint(len(far))]
    return np.exp2(a.ravel()).repeat(32)


def f64(x):
    return np.asarray(x).astype(np.float64)


def striped(idx):
    return np.tile(idx.reshape(-1, 16).T, (8, 1)).astype(np.uint16)


def unstriped(offs):
    return offs[:16].T.reshape(-1).astype(np.int64)


E2M1 = np.array([0.0, 0.5, 1.0, 1.5, 2.0, 3.0, 4.0, 6.0, -0.0, -0.5, -1.0, -1.5, -2.0, -3.0, -4.0, -6.0])


def pack_weight(w, fmt):
    k, n = w.shape
    w = f64(np.asarray(w, np.float32).astype(ml_dtypes.bfloat16)).reshape(k // 32, 32, n)
    amax = np.abs(w).max(1)
    if fmt == "e4m3":
        byte = np.frexp(amax)[1] - 1 + 127 - 7
    else:
        mant, ex = np.frexp(amax / 6.0)
        byte = np.where(mant > 0.5, ex, ex - 1) + 127
    byte = np.clip(np.where(amax > 0, byte, 1), 1, 254)
    scaled = (w * np.exp2(127.0 - byte)[:, None, :]).reshape(k, n).astype(np.float32)
    by_word = np.ascontiguousarray(scaled.reshape(k // 512, 128, 4, n).transpose(0, 1, 3, 2))
    if fmt == "e4m3":
        words = by_word.astype(ml_dtypes.float8_e4m3fn).view(np.uint8)
    else:
        c = by_word.astype(ml_dtypes.float4_e2m1fn).view(np.uint8) & 0xF
        words = (c[..., 0::2] | (c[..., 1::2] << 4)).reshape(k // 512, 128, 2 * n)
    return np.ascontiguousarray(words), np.ascontiguousarray(byte.astype(np.uint8).reshape(k // 512, 16, n))


def unpack_weight(words, scales, fmt):
    g, _, n = scales.shape
    words = np.ascontiguousarray(words).reshape(g, 128, n, -1)
    if fmt == "e4m3":
        vals = words.view(ml_dtypes.float8_e4m3fn).astype(np.float64)
    else:
        nib = np.empty((g, 128, n, 4), np.uint8)
        nib[..., 0::2] = words & 0xF
        nib[..., 1::2] = words >> 4
        vals = E2M1[nib]
    vals = vals * np.repeat(np.exp2(scales.astype(np.float64) - 127.0), 8, axis=1)[..., None]
    return vals.transpose(0, 1, 3, 2).reshape(g * 512, n)


def gelu(v):
    return 0.5 * v * (1.0 + np.tanh(np.sqrt(2.0 / np.pi) * (v + 0.044715 * v**3)))


def striped8(idx):
    return np.concatenate([v.reshape(-1, 16).T for v in idx]).astype(np.uint16)


def unstriped8(offs):
    return np.stack([offs[16 * g:16 * g + 16].T.reshape(-1) for g in range(8)]).astype(np.int64)


def heads(h, wgt, idx8):
    r = np.arange(h.shape[0])
    return wgt[r // 4 % 128] * h[r[:, None], idx8[r % 512 // 64]]


def put_heads(h, wgs, idx8, t2):
    r = np.arange(h.shape[0])
    page = np.zeros((h.shape[0], t2))
    page[r[:, None], idx8[r % 512 // 64]] = wgs[r // 4 % 128] * h
    return page


K, H, N, T, S, P, T2 = 1024, 1024, 512, 4096, 1024, 512, 1024

def setup_inputs():
    n = np.random.standard_normal
    s = mx_kscale(K)[:, None]
    u = mx_kscale(H)[:, None]
    d = {}
    d["tab_words"], d["tab_scales"] = pack_weight(n((K, T)) * s, "e4m3")
    d["offs"] = striped(np.random.permutation(T)[:S])
    d["w1"] = (n((K, H)) / s / K ** 0.5).astype(np.float32)
    d["offs2"] = striped8(np.stack([np.random.permutation(S)[:P] for _ in range(8)]))
    d["wgt"] = np.repeat(np.random.uniform(0.5, 2.0, (8, P)), 16, axis=0).astype(np.float32)
    d["b1"] = (0.5 * n(H)).astype(np.float32)
    d["gain"] = (np.exp(0.3 * n(H)) * u[:, 0]).astype(np.float32)
    d["w4_words"], d["w4_scales"] = pack_weight(2.0 * n((H, N)) / u / H ** 0.5, "e2m1")
    d["tmpl"] = (n((K, P)) * s).astype(np.float32)
    d["w3"] = (1.3 * n((K, N)) / s / K ** 0.5).astype(np.float32)
    d["b3"] = (0.5 * n(N)).astype(np.float32)
    d["offs3"] = striped8(np.stack([np.random.permutation(T2)[:P] for _ in range(8)]))
    d["wgo"] = np.repeat(np.random.uniform(0.5, 2.0, (8, P)), 16, axis=0).astype(np.float32)
    return d

def reference(tab_words, tab_scales, offs, w1, offs2, wgt, b1, gain, w4_words, w4_scales, tmpl, w3, b3, offs3, wgo):
    v = unpack_weight(tab_words, tab_scales, "e4m3")[:, unstriped(offs)]
    h = mxq(f64(w1), 0, "e4m3").T @ v
    x = heads(h, f64(wgt), unstriped8(offs2))
    z = np.tanh(x + f64(b1)[:, None]) * f64(gain)[:, None]
    w4 = unpack_weight(w4_words, w4_scales, "e2m1")
    f = w4.T @ mxq(z, 0, "e4m3")
    t = mxq(f64(w3), 0, "e4m3").T @ mxq(f64(tmpl), 0, "e4m3")
    y = f * np.tanh(t + f64(b3)[:, None])
    return put_heads(y, f64(wgo), unstriped8(offs3), T2)

@@ -1,0 +1,281 @@
+from contextlib import ExitStack
+
+import concourse.mybir as mybir
+
+K, H, N, T, S, M, T2 = 1024, 1024, 512, 4096, 1024, 512, 1024
+FLOPS = 2 * (K * H * S + H * N * M + K * N * M)
+
+F32 = mybir.dt.float32
+BF16 = mybir.dt.bfloat16
+I32 = mybir.dt.int32
+U32 = mybir.dt.uint32
+U16 = mybir.dt.uint16
+U8 = mybir.dt.uint8
+FP8X4 = mybir.dt.float8_e4m3fn_x4
+FP4X4 = mybir.dt.float4_e2m1fn_x4
+MULT = mybir.AluOpType.mult
+TANH = mybir.ActivationFunctionType.Tanh
+COPY = mybir.ActivationFunctionType.Copy
+
+P = 128
+PACK = 4
+KP = P * PACK
+HALF = M // 2
+
+
+def tile_list_braille_fault_scores_kernel(
+    tc, tab_words, tab_scales, offs, w1, offs2, wgt, b1, gain, w4_words, w4_scales, tmpl, w3, b3, offs3, wgo, out
+):
+    nc = tc.nc
+    with ExitStack() as ctx:
+        keep = ctx.enter_context(tc.tile_pool(name="keep", bufs=1))
+        ring = ctx.enter_context(tc.tile_pool(name="ring", bufs=2))
+        psum = ctx.enter_context(tc.psum_pool(name="psum", bufs=8))
+
+        list1 = keep.tile([P, S // 16], U16, name="list1")
+        list2 = keep.tile([P, M // 16], U16, name="list2")
+        list3 = keep.tile([P, M // 16], U16, name="list3")
+        tab_w = [keep.tile([P, T], U32, name="tab_w%d" % a) for a in range(2)]
+        tab_s = keep.tile([P, T], U8, name="tab_s")
+        w4_w = keep.tile([P, 2, 2 * N], U8, name="w4_w")
+        w4_s = keep.tile([P, 2, N], U8, name="w4_s")
+        wgt_t = keep.tile([P, M], F32, name="wgt_t")
+        wgo_t = keep.tile([P, M], F32, name="wgo_t")
+        b1_t = keep.tile([P, 2, PACK], F32, name="b1_t")
+        gain_t = keep.tile([P, 2, PACK], F32, name="gain_t")
+        b3_t = keep.tile([P, PACK], F32, name="b3_t")
+        pages = [keep.tile([P, T2], F32, name="page%d" % i) for i in range(PACK)]
+        warm_in = keep.tile([P, 1], F32, name="warm_in")
+        warm_out = keep.tile([P, 1], F32, name="warm_out")
+
+        nc.vector.memset(tab_s[:].bitcast(I32), 0)
+        nc.vector.memset(warm_in[:], 0.0)
+        nc.scalar.activation(warm_out[:], warm_in[:], TANH)
+        nc.vector.memset(w4_s[:].rearrange("p a c -> p (a c)").bitcast(I32), 0)
+        for page in pages:
+            nc.vector.memset(page[:], 0.0)
+
+        def load_rows(src, a, c0, name):
+            raw = ring.tile([P, PACK, KP], F32, name=name, tag="raw", bufs=6)
+            nc.sync.dma_start(raw[:], src[a * KP : (a + 1) * KP, c0 : c0 + KP].rearrange("(p j) c -> p j c", j=PACK))
+            return raw
+
+        nc.sync.dma_start(list1[:], offs)
+        for q in range(4):
+            nc.gpsimd.dma_start(tab_s[32 * q : 32 * q + 8, :].bitcast(I32), tab_scales[:, 4 * q : 4 * q + 4, :].bitcast(I32))
+        for a in range(2):
+            nc.sync.dma_start(tab_w[a][:].bitcast(I32), tab_words[a].rearrange("p t i -> p (t i)").bitcast(I32))
+        w1_raw = {}
+        for a in range(2):
+            w1_raw[0, a] = load_rows(w1, a, 0, "w1_0%d" % a)
+        nc.sync.dma_start(list2[:], offs2)
+        nc.sync.dma_start(wgt_t[:], wgt)
+        nc.sync.dma_start(w4_w[:].bitcast(I32), w4_words.rearrange("a p c -> p a c").bitcast(I32))
+        nc.scalar.dma_start(b1_t[:], b1.rearrange("(b p i) -> p b i", b=2, i=PACK))
+        nc.scalar.dma_start(gain_t[:], gain.rearrange("(b p i) -> p b i", b=2, i=PACK))
+        nc.scalar.dma_start(b3_t[:], b3.rearrange("(p i) -> p i", i=PACK))
+        for q in range(4):
+            nc.gpsimd.dma_start(
+                w4_s[32 * q : 32 * q + 4, :, :].bitcast(I32),
+                w4_scales[:, 4 * q : 4 * q + 4, :].rearrange("a r c -> r a c").bitcast(I32),
+            )
+        for a in range(2):
+            w1_raw[1, a] = load_rows(w1, a, KP, "w1_1%d" % a)
+        w3_raw = [load_rows(w3, a, 0, "w3_%d" % a) for a in range(2)]
+        tmpl_raw = [load_rows(tmpl, a, 0, "tmpl_%d" % a) for a in range(2)]
+        nc.sync.dma_start(list3[:], offs3)
+        nc.sync.dma_start(wgo_t[:], wgo)
+
+        def copy_on(engine, dst, src):
+            if engine == "v":
+                nc.vector.tensor_copy(dst, src)
+            else:
+                nc.scalar.copy(dst, src)
+
+        def quantise(grouped, name):
+            codes = keep.tile([P, 256], U32, name=name + "_codes", align_bytes=64)
+            scales = keep.tile([P, 256], U8, name=name + "_scales", align_bytes=64)
+            nc.vector.quantize_mx(out=codes[:].bitcast(FP8X4), scales=scales[:], in_=grouped[:])
+            return codes, scales
+
+        def new_grouped(name):
+            return ring.tile([P, 256 * PACK], BF16, name=name, tag="grouped", bufs=8, align_bytes=64)
+
+        def cast_weight(engine, raw, pair, name):
+            grouped = new_grouped(name)
+            copy_on(
+                engine,
+                grouped[:].rearrange("p (t q j) -> p q j t", t=2, j=PACK),
+                raw[:].rearrange("p j (q t) -> p q j t", t=PACK)[:, :, :, 2 * pair : 2 * pair + 2],
+            )
+            return grouped
+
+        def interleave_views(grouped, rows):
+            return (
+                grouped[:].rearrange("p (c u j) -> p c j u", u=4, j=PACK),
+                rows.rearrange("p j (c u) -> p c j u", u=4),
+            )
+
+        def cast_moving(engine, rows, name):
+            grouped = new_grouped(name)
+            dst, src = interleave_views(grouped, rows)
+            copy_on(engine, dst, src)
+            return grouped
+
+        def mm(acc, lhs, slot, rhs_codes, rhs_scales, a):
+            cols = slice(P * (slot % 2), P * (slot % 2 + 1))
+            nc.tensor.matmul_mx(
+                out=acc, lhsT=lhs[0][:, cols].bitcast(FP8X4), lhsT_scale=lhs[1][:, cols],
+                rhs=rhs_codes.bitcast(FP8X4), rhs_scale=rhs_scales, start=(a == 0), stop=(a == 1),
+            )
+
+        v_s = keep.tile([P, S], U8, name="v_s", align_bytes=64)
+        v_w = [keep.tile([P, S], U32, name="v_w%d" % a, align_bytes=64) for a in range(2)]
+        nc.vector.tensor_copy(v_s[:], tab_s[:].indirect(list1[:]))
+        for a in range(2):
+            nc.vector.tensor_copy(v_w[a][:], tab_w[a][:].indirect(list1[:]))
+
+        w1_q = {}
+
+        def prepare_w1(b, a, engines):
+            casts = [cast_weight(engines[pair], w1_raw[b, a], pair, "g_w1_%d%d%d" % (b, a, pair)) for pair in range(2)]
+            for pair in range(2):
+                w1_q[b, a, pair] = quantise(casts[pair], "w1_%d%d%d" % (b, a, pair))
+
+        h = {}
+
+        def make_h(b, i, engines):
+            h[b, i] = ring.tile([P, S], F32, name="h%d%d" % (b, i), tag="h", bufs=4)
+            for c in range(2):
+                cols = slice(c * KP, (c + 1) * KP)
+                acc = psum.tile([P, KP], F32, name="h_acc%d%d%d" % (b, i, c), tag="bank")
+                for a in range(2):
+                    mm(acc[:], w1_q[b, a, i // 2], i, v_w[a][:, cols], v_s[4 * a : P, cols], a)
+                copy_on(engines[c], h[b, i][:, cols], acc[:])
+
+        th = {}
+
+        def pick(b, i, halves):
+            width = HALF * len(halves)
+            m0 = HALF * halves[0]
+            x = ring.tile([P, width], F32, name="x%d%d%d" % (b, i, halves[0]), tag="x", bufs=8)
+            nc.vector.tensor_tensor(
+                x[:], h[b, i][:].indirect(list2[:, m0 // 16 : (m0 + width) // 16]), wgt_t[:, m0 : m0 + width], MULT
+            )
+            return x
+
+        def squash(b, i, halves, x):
+            width = HALF * len(halves)
+            if i == 0:
+                rows = keep.tile([P, PACK, width], F32, name="th%d%d" % (b, halves[0]))
+                th[b, "rows", halves[0]] = rows
+                for n, half in enumerate(halves):
+                    th[b, half] = rows[:, :, n * HALF : (n + 1) * HALF]
+            nc.scalar.activation(th[b, "rows", halves[0]][:, i, :], x[:], TANH, bias=b1_t[:, b, i : i + 1])
+
+        z_q = {}
+
+        def make_z(b, half, engine):
+            grouped = new_grouped("g_z%d%d" % (b, half))
+            if engine == "v":
+                dst, src = interleave_views(grouped, th[b, half])
+                g = gain_t[:, b, :].unsqueeze(1).unsqueeze(3).to_broadcast([P, HALF // 4, PACK, 4])
+                nc.vector.tensor_tensor(dst, src, g, MULT)
+            else:
+                zr = ring.tile([P, PACK, HALF], BF16, name="zr%d%d" % (b, half), tag="zr")
+                for i in range(PACK):
+                    nc.scalar.activation(zr[:, i, :], th[b, half][:, i, :], COPY, scale=gain_t[:, b, i : i + 1])
+                dst, src = interleave_views(grouped, zr[:])
+                nc.vector.tensor_copy(dst, src)
+            z_q[b, half] = quantise(grouped, "z%d%d" % (b, half))
+
+        prepare_w1(0, 0, "ss")
+        prepare_w1(0, 1, "vs")
+        make_h(0, 0, "vs")
+        for i in range(1, PACK):
+            make_h(0, i, "ss")
+
+        w4_wd = keep.tile([P, 2, 2 * N], U8, name="w4_wd", align_bytes=64)
+        w4_sd = keep.tile([P, 2, N], U8, name="w4_sd", align_bytes=64)
+
+        xs = [pick(0, i, [0, 1]) for i in range(2)]
+        prepare_w1(1, 0, "vv")
+        prepare_w1(1, 1, "vv")
+        xs += [pick(0, i, [0, 1]) for i in range(2, PACK)]
+        for i in range(PACK):
+            make_h(1, i, "ss")
+        for i in range(PACK):
+            squash(0, i, [0, 1], xs[i])
+        xa = [pick(1, i, [0]) for i in range(PACK)]
+        for i in range(PACK):
+            squash(1, i, [0], xa[i])
+        xb = [pick(1, i, [1]) for i in range(PACK)]
+        make_z(0, 0, "v")
+        make_z(1, 0, "v")
+
+        nc.vector.tensor_copy(
+            w4_wd[:].bitcast(U16).rearrange("p a (t q) -> p a q t", t=PACK),
+            w4_w[:].bitcast(U16).rearrange("p a (q t) -> p a q t", t=PACK),
+        )
+        nc.vector.tensor_copy(
+            w4_sd[:].rearrange("p a (t q) -> p a q t", t=PACK), w4_s[:].rearrange("p a (q t) -> p a q t", t=PACK)
+        )
+
+        w3_q, tmpl_q = {}, {}
+        for a in range(2):
+            for pair in range(2):
+                w3_q[a, pair] = quantise(cast_weight("s", w3_raw[a], pair, "g_w3_%d%d" % (a, pair)), "w3_%d%d" % (a, pair))
+
+        tt = {}
+
+        def make_t(half):
+            cols = slice(half * HALF, (half + 1) * HALF)
+            for a in range(2):
+                tmpl_q[a, half] = quantise(
+                    cast_moving("s", tmpl_raw[a][:, :, cols], "g_tm%d%d" % (a, half)), "tm%d%d" % (a, half)
+                )
+            for pair in range(2):
+                acc = psum.tile([P, 2, HALF], F32, name="t_acc%d%d" % (half, pair), tag="bank")
+                tt[half, pair] = keep.tile([P, 2, HALF], F32, name="tt%d%d" % (half, pair))
+                for s in range(2):
+                    for a in range(2):
+                        mm(acc[:, s, :], w3_q[a, pair], s, tmpl_q[a, half][0][:], tmpl_q[a, half][1][:], a)
+                for s in range(2):
+                    i = 2 * pair + s
+                    nc.scalar.activation(tt[half, pair][:, s, :], acc[:, s, :], TANH, bias=b3_t[:, i : i + 1])
+
+        def make_out(half):
+            cols = slice(half * HALF, (half + 1) * HALF)
+            ys = []
+            for pair in range(2):
+                acc = psum.tile([P, 2, HALF], F32, name="f_acc%d%d" % (half, pair), tag="bank")
+                for s in range(2):
+                    i = 2 * pair + s
+                    for c in range(2):
+                        part = slice(c * P, (c + 1) * P)
+                        for b in range(2):
+                            nc.tensor.matmul_mx(
+                                out=acc[:, s, part],
+                                lhsT=w4_wd[:, b, 2 * P * i : 2 * P * (i + 1)].bitcast(FP4X4),
+                                lhsT_scale=w4_sd[:, b, P * i : P * (i + 1)],
+                                rhs=z_q[b, half][0][:, part].bitcast(FP8X4),
+                                rhs_scale=z_q[b, half][1][:, part],
+                                start=(b == 0), stop=(b == 1),
+                            )
+                y = ring.tile([P, 2, HALF], F32, name="y%d%d" % (half, pair), tag="y")
+                nc.vector.tensor_tensor(y[:], acc[:], tt[half, pair][:], MULT)
+                ys.append(y)
+            for i in range(PACK):
+                window = pages[i][:].indirect(list3[:, half * HALF // 16 : (half + 1) * HALF // 16])
+                nc.vector.tensor_tensor(window, ys[i // 2][:, i % 2, :], wgo_t[:, cols], MULT)
+                if half == 1:
+                    nc.sync.dma_start(out.rearrange("(p i) c -> p i c", i=PACK)[:, i, :], pages[i][:])
+
+        make_t(0)
+        make_out(0)
+        for i in range(PACK):
+            squash(1, i, [1], xb[i])
+        make_z(0, 1, "s")
+        make_z(1, 1, "s")
+        make_t(1)
+        make_out(1)

@@ -21,6 +21,7 @@ P = 128
 PACK = 4
 KP = P * PACK
 HALF = M // 2
+XB = {256: 4, 512: 4}
 
 
 def tile_list_braille_fault_scores_kernel(
@@ -29,14 +30,13 @@ def tile_list_braille_fault_scores_kernel(
     nc = tc.nc
     with ExitStack() as ctx:
         keep = ctx.enter_context(tc.tile_pool(name="keep", bufs=1))
-        ring = ctx.enter_context(tc.tile_pool(name="ring", bufs=2))
         psum = ctx.enter_context(tc.psum_pool(name="psum", bufs=8))
 
         list1 = keep.tile([P, S // 16], U16, name="list1")
         list2 = keep.tile([P, M // 16], U16, name="list2")
         list3 = keep.tile([P, M // 16], U16, name="list3")
         tab_w = [keep.tile([P, T], U32, name="tab_w%d" % a) for a in range(2)]
-        tab_s = keep.tile([P, T], U8, name="tab_s")
+        tab_s = keep.tile([P, T], U8, name="tab_s", tag="w1_00_codes", align_bytes=64)
         w4_w = keep.tile([P, 2, 2 * N], U8, name="w4_w")
         w4_s = keep.tile([P, 2, N], U8, name="w4_s")
         wgt_t = keep.tile([P, M], F32, name="wgt_t")
@@ -50,41 +50,54 @@ def tile_list_braille_fault_scores_kernel(
 
         nc.vector.memset(tab_s[:].bitcast(I32), 0)
         nc.vector.memset(warm_in[:], 0.0)
-        nc.scalar.activation(warm_out[:], warm_in[:], TANH)
-        nc.vector.memset(w4_s[:].rearrange("p a c -> p (a c)").bitcast(I32), 0)
+        nc.gpsimd.memset(w4_s[:].rearrange("p a c -> p (a c)").bitcast(I32), 0)
         for page in pages:
             nc.vector.memset(page[:], 0.0)
 
-        def load_rows(src, a, c0, name):
-            raw = ring.tile([P, PACK, KP], F32, name=name, tag="raw", bufs=6)
-            nc.sync.dma_start(raw[:], src[a * KP : (a + 1) * KP, c0 : c0 + KP].rearrange("(p j) c -> p j c", j=PACK))
+        def load_rows(src, a, c0, width, name, tag):
+            raw = keep.tile([P, PACK, width], F32, name=name, tag=tag, align_bytes=64)
+            rows = src[a * KP : (a + 1) * KP, c0 : c0 + width]
+            nc.sync.dma_start(raw[:], rows.rearrange("(p j) c -> p j c", j=PACK))
             return raw
 
-        nc.sync.dma_start(list1[:], offs)
-        for q in range(4):
-            nc.gpsimd.dma_start(tab_s[32 * q : 32 * q + 8, :].bitcast(I32), tab_scales[:, 4 * q : 4 * q + 4, :].bitcast(I32))
-        for a in range(2):
-            nc.sync.dma_start(tab_w[a][:].bitcast(I32), tab_words[a].rearrange("p t i -> p (t i)").bitcast(I32))
+        def load_table(a, cols):
+            words = tab_words[a].rearrange("p t i -> p (t i)").bitcast(I32)
+            nc.sync.dma_start(tab_w[a][:].bitcast(I32)[:, cols], words[:, cols])
+
         w1_raw = {}
-        for a in range(2):
-            w1_raw[0, a] = load_rows(w1, a, 0, "w1_0%d" % a)
-        nc.sync.dma_start(list2[:], offs2)
-        nc.sync.dma_start(wgt_t[:], wgt)
+        nc.sync.dma_start(list1[:], offs)
+        nc.scalar.activation(warm_out[:], warm_in[:], TANH)
         nc.sync.dma_start(w4_w[:].bitcast(I32), w4_words.rearrange("a p c -> p a c").bitcast(I32))
-        nc.scalar.dma_start(b1_t[:], b1.rearrange("(b p i) -> p b i", b=2, i=PACK))
-        nc.scalar.dma_start(gain_t[:], gain.rearrange("(b p i) -> p b i", b=2, i=PACK))
-        nc.scalar.dma_start(b3_t[:], b3.rearrange("(p i) -> p i", i=PACK))
         for q in range(4):
-            nc.gpsimd.dma_start(
+            nc.sync.dma_start(
                 w4_s[32 * q : 32 * q + 4, :, :].bitcast(I32),
                 w4_scales[:, 4 * q : 4 * q + 4, :].rearrange("a r c -> r a c").bitcast(I32),
             )
+        load_table(0, slice(0, T // 2))
+        load_table(0, slice(T // 2, T))
+        for n in range(8):
+            a, q = divmod(n, 4)
+            if n == 6:
+                w1_raw[0, 0] = load_rows(w1, 0, 0, KP, "w1_00", "raw0")
+            row = 32 * q + 4 * a
+            nc.sync.dma_start(tab_s[row : row + 4, :].bitcast(I32), tab_scales[a, 4 * q : 4 * q + 4, :].bitcast(I32))
+        load_table(1, slice(0, T))
+        w1_raw[0, 1] = load_rows(w1, 1, 0, KP, "w1_01", "raw1")
+        nc.sync.dma_start(list2[:], offs2)
+        nc.sync.dma_start(wgt_t[:], wgt)
+        nc.sync.dma_start(b1_t[:], b1.rearrange("(b p i) -> p b i", b=2, i=PACK))
         for a in range(2):
-            w1_raw[1, a] = load_rows(w1, a, KP, "w1_1%d" % a)
-        w3_raw = [load_rows(w3, a, 0, "w3_%d" % a) for a in range(2)]
-        tmpl_raw = [load_rows(tmpl, a, 0, "tmpl_%d" % a) for a in range(2)]
+            w1_raw[1, a] = load_rows(w1, a, KP, KP, "w1_1%d" % a, "raw%d" % (2 + a))
+        w3_raw = [load_rows(w3, a, 0, KP, "w3_%d" % a, "raw%d" % (4 + a)) for a in range(2)]
+        nc.sync.dma_start(gain_t[:], gain.rearrange("(b p i) -> p b i", b=2, i=PACK))
+        tmpl_raw = {}
+        for a in range(2):
+            tmpl_raw[a, 0] = load_rows(tmpl, a, 0, HALF, "tmpl_%d0" % a, "tma%d" % a)
         nc.sync.dma_start(list3[:], offs3)
+        nc.sync.dma_start(b3_t[:], b3.rearrange("(p i) -> p i", i=PACK))
         nc.sync.dma_start(wgo_t[:], wgo)
+        for a in range(2):
+            tmpl_raw[a, 1] = load_rows(tmpl, a, HALF, HALF, "tmpl_%d1" % a, "raw%d" % (2 + a))
 
         def copy_on(engine, dst, src):
             if engine == "v":
@@ -92,127 +105,43 @@ def tile_list_braille_fault_scores_kernel(
             else:
                 nc.scalar.copy(dst, src)
 
-        def quantise(grouped, name):
-            codes = keep.tile([P, 256], U32, name=name + "_codes", align_bytes=64)
-            scales = keep.tile([P, 256], U8, name=name + "_scales", align_bytes=64)
+        def quantise(grouped, width, name):
+            codes = keep.tile([P, width], U32, name=name + "_codes", align_bytes=64)
+            scales = keep.tile([P, width], U8, name=name + "_scales", align_bytes=64)
             nc.vector.quantize_mx(out=codes[:].bitcast(FP8X4), scales=scales[:], in_=grouped[:])
             return codes, scales
 
-        def new_grouped(name):
-            return ring.tile([P, 256 * PACK], BF16, name=name, tag="grouped", bufs=8, align_bytes=64)
+        def new_grouped(width, name, tag):
+            return keep.tile([P, width * PACK], BF16, name=name, tag=tag, align_bytes=64)
 
-        def cast_weight(engine, raw, pair, name):
-            grouped = new_grouped(name)
+        def cast_weight(engine, raw, slots, name, tag):
+            grouped = new_grouped(P * len(slots), name, tag)
             copy_on(
                 engine,
-                grouped[:].rearrange("p (t q j) -> p q j t", t=2, j=PACK),
-                raw[:].rearrange("p j (q t) -> p q j t", t=PACK)[:, :, :, 2 * pair : 2 * pair + 2],
+                grouped[:].rearrange("p (t q j) -> p q j t", t=len(slots), j=PACK),
+                raw[:].rearrange("p j (q t) -> p q j t", t=PACK)[:, :, :, slots[0] : slots[-1] + 1],
             )
             return grouped
+
+        def quantise_weight(grouped, slots, name, into, key):
+            codes, scales = quantise(grouped, P * len(slots), name)
+            for n, slot in enumerate(slots):
+                into[key + (slot,)] = (codes[:, n * P : (n + 1) * P], scales[:, n * P : (n + 1) * P])
 
         def interleave_views(grouped, rows):
             return (
-                grouped[:].rearrange("p (c u j) -> p c j u", u=4, j=PACK),
+                grouped.rearrange("p (c u j) -> p c j u", u=4, j=PACK),
                 rows.rearrange("p j (c u) -> p c j u", u=4),
             )
 
-        def cast_moving(engine, rows, name):
-            grouped = new_grouped(name)
-            dst, src = interleave_views(grouped, rows)
-            copy_on(engine, dst, src)
-            return grouped
-
-        def mm(acc, lhs, slot, rhs_codes, rhs_scales, a):
-            cols = slice(P * (slot % 2), P * (slot % 2 + 1))
+        def mm(acc, lhs, rhs_codes, rhs_scales, a):
             nc.tensor.matmul_mx(
-                out=acc, lhsT=lhs[0][:, cols].bitcast(FP8X4), lhsT_scale=lhs[1][:, cols],
+                out=acc, lhsT=lhs[0].bitcast(FP8X4), lhsT_scale=lhs[1],
                 rhs=rhs_codes.bitcast(FP8X4), rhs_scale=rhs_scales, start=(a == 0), stop=(a == 1),
             )
 
-        v_s = keep.tile([P, S], U8, name="v_s", align_bytes=64)
-        v_w = [keep.tile([P, S], U32, name="v_w%d" % a, align_bytes=64) for a in range(2)]
-        nc.vector.tensor_copy(v_s[:], tab_s[:].indirect(list1[:]))
-        for a in range(2):
-            nc.vector.tensor_copy(v_w[a][:], tab_w[a][:].indirect(list1[:]))
-
-        w1_q = {}
-
-        def prepare_w1(b, a, engines):
-            casts = [cast_weight(engines[pair], w1_raw[b, a], pair, "g_w1_%d%d%d" % (b, a, pair)) for pair in range(2)]
-            for pair in range(2):
-                w1_q[b, a, pair] = quantise(casts[pair], "w1_%d%d%d" % (b, a, pair))
-
-        h = {}
-
-        def make_h(b, i, engines):
-            h[b, i] = ring.tile([P, S], F32, name="h%d%d" % (b, i), tag="h", bufs=4)
-            for c in range(2):
-                cols = slice(c * KP, (c + 1) * KP)
-                acc = psum.tile([P, KP], F32, name="h_acc%d%d%d" % (b, i, c), tag="bank")
-                for a in range(2):
-                    mm(acc[:], w1_q[b, a, i // 2], i, v_w[a][:, cols], v_s[4 * a : P, cols], a)
-                copy_on(engines[c], h[b, i][:, cols], acc[:])
-
-        th = {}
-
-        def pick(b, i, halves):
-            width = HALF * len(halves)
-            m0 = HALF * halves[0]
-            x = ring.tile([P, width], F32, name="x%d%d%d" % (b, i, halves[0]), tag="x", bufs=8)
-            nc.vector.tensor_tensor(
-                x[:], h[b, i][:].indirect(list2[:, m0 // 16 : (m0 + width) // 16]), wgt_t[:, m0 : m0 + width], MULT
-            )
-            return x
-
-        def squash(b, i, halves, x):
-            width = HALF * len(halves)
-            if i == 0:
-                rows = keep.tile([P, PACK, width], F32, name="th%d%d" % (b, halves[0]))
-                th[b, "rows", halves[0]] = rows
-                for n, half in enumerate(halves):
-                    th[b, half] = rows[:, :, n * HALF : (n + 1) * HALF]
-            nc.scalar.activation(th[b, "rows", halves[0]][:, i, :], x[:], TANH, bias=b1_t[:, b, i : i + 1])
-
-        z_q = {}
-
-        def make_z(b, half, engine):
-            grouped = new_grouped("g_z%d%d" % (b, half))
-            if engine == "v":
-                dst, src = interleave_views(grouped, th[b, half])
-                g = gain_t[:, b, :].unsqueeze(1).unsqueeze(3).to_broadcast([P, HALF // 4, PACK, 4])
-                nc.vector.tensor_tensor(dst, src, g, MULT)
-            else:
-                zr = ring.tile([P, PACK, HALF], BF16, name="zr%d%d" % (b, half), tag="zr")
-                for i in range(PACK):
-                    nc.scalar.activation(zr[:, i, :], th[b, half][:, i, :], COPY, scale=gain_t[:, b, i : i + 1])
-                dst, src = interleave_views(grouped, zr[:])
-                nc.vector.tensor_copy(dst, src)
-            z_q[b, half] = quantise(grouped, "z%d%d" % (b, half))
-
-        prepare_w1(0, 0, "ss")
-        prepare_w1(0, 1, "vs")
-        make_h(0, 0, "vs")
-        for i in range(1, PACK):
-            make_h(0, i, "ss")
-
         w4_wd = keep.tile([P, 2, 2 * N], U8, name="w4_wd", align_bytes=64)
         w4_sd = keep.tile([P, 2, N], U8, name="w4_sd", align_bytes=64)
-
-        xs = [pick(0, i, [0, 1]) for i in range(2)]
-        prepare_w1(1, 0, "vv")
-        prepare_w1(1, 1, "vv")
-        xs += [pick(0, i, [0, 1]) for i in range(2, PACK)]
-        for i in range(PACK):
-            make_h(1, i, "ss")
-        for i in range(PACK):
-            squash(0, i, [0, 1], xs[i])
-        xa = [pick(1, i, [0]) for i in range(PACK)]
-        for i in range(PACK):
-            squash(1, i, [0], xa[i])
-        xb = [pick(1, i, [1]) for i in range(PACK)]
-        make_z(0, 0, "v")
-        make_z(1, 0, "v")
-
         nc.vector.tensor_copy(
             w4_wd[:].bitcast(U16).rearrange("p a (t q) -> p a q t", t=PACK),
             w4_w[:].bitcast(U16).rearrange("p a (q t) -> p a q t", t=PACK),
@@ -221,61 +150,145 @@ def tile_list_braille_fault_scores_kernel(
             w4_sd[:].rearrange("p a (t q) -> p a q t", t=PACK), w4_s[:].rearrange("p a (q t) -> p a q t", t=PACK)
         )
 
-        w3_q, tmpl_q = {}, {}
-        for a in range(2):
-            for pair in range(2):
-                w3_q[a, pair] = quantise(cast_weight("s", w3_raw[a], pair, "g_w3_%d%d" % (a, pair)), "w3_%d%d" % (a, pair))
+        v_s = keep.tile([P, S], U8, name="v_s", align_bytes=64)
+        v_w = [keep.tile([P, S], U32, name="v_w0", align_bytes=64)]
+        nc.vector.tensor_copy(v_w[0][:], tab_w[0][:].indirect(list1[:]))
+        nc.vector.tensor_copy(v_s[:], tab_s[:].indirect(list1[:]))
+        w1_q, w3_q = {}, {}
+        ALL, LO, HI = [0, 1, 2, 3], [0, 1], [2, 3]
+        quantise_weight(cast_weight("s", w1_raw[0, 0], ALL, "g_w1_00", "vw1"), ALL, "w1_00", w1_q, (0, 0))
+        v_w.append(keep.tile([P, S], U32, name="v_w1", tag="vw1", align_bytes=64))
+        nc.vector.tensor_copy(v_w[1][:], tab_w[1][:].indirect(list1[:]))
+        lo = cast_weight("v", w1_raw[0, 1], LO, "g_w1_01l", "g1")
+        hi = cast_weight("s", w1_raw[0, 1], HI, "g_w1_01h", "g2")
+        quantise_weight(lo, LO, "w1_01l", w1_q, (0, 1))
+        quantise_weight(hi, HI, "w1_01h", w1_q, (0, 1))
 
-        tt = {}
+        h = {}
 
-        def make_t(half):
-            cols = slice(half * HALF, (half + 1) * HALF)
-            for a in range(2):
-                tmpl_q[a, half] = quantise(
-                    cast_moving("s", tmpl_raw[a][:, :, cols], "g_tm%d%d" % (a, half)), "tm%d%d" % (a, half)
-                )
-            for pair in range(2):
-                acc = psum.tile([P, 2, HALF], F32, name="t_acc%d%d" % (half, pair), tag="bank")
-                tt[half, pair] = keep.tile([P, 2, HALF], F32, name="tt%d%d" % (half, pair))
-                for s in range(2):
-                    for a in range(2):
-                        mm(acc[:, s, :], w3_q[a, pair], s, tmpl_q[a, half][0][:], tmpl_q[a, half][1][:], a)
-                for s in range(2):
-                    i = 2 * pair + s
-                    nc.scalar.activation(tt[half, pair][:, s, :], acc[:, s, :], TANH, bias=b3_t[:, i : i + 1])
+        def make_h(b, i, engines):
+            h[b, i] = keep.tile([P, S], F32, name="h%d%d" % (b, i), tag="h", bufs=5)
+            for c in range(2):
+                cols = slice(c * KP, (c + 1) * KP)
+                acc = psum.tile([P, KP], F32, name="h_acc%d%d%d" % (b, i, c), tag="bank")
+                for a in range(2):
+                    mm(acc[:], w1_q[b, a, i], v_w[a][:, cols], v_s[4 * a : P, cols], a)
+                copy_on(engines[c], h[b, i][:, cols], acc[:])
 
-        def make_out(half):
-            cols = slice(half * HALF, (half + 1) * HALF)
-            ys = []
-            for pair in range(2):
-                acc = psum.tile([P, 2, HALF], F32, name="f_acc%d%d" % (half, pair), tag="bank")
-                for s in range(2):
-                    i = 2 * pair + s
-                    for c in range(2):
-                        part = slice(c * P, (c + 1) * P)
-                        for b in range(2):
-                            nc.tensor.matmul_mx(
-                                out=acc[:, s, part],
-                                lhsT=w4_wd[:, b, 2 * P * i : 2 * P * (i + 1)].bitcast(FP4X4),
-                                lhsT_scale=w4_sd[:, b, P * i : P * (i + 1)],
-                                rhs=z_q[b, half][0][:, part].bitcast(FP8X4),
-                                rhs_scale=z_q[b, half][1][:, part],
-                                start=(b == 0), stop=(b == 1),
-                            )
-                y = ring.tile([P, 2, HALF], F32, name="y%d%d" % (half, pair), tag="y")
-                nc.vector.tensor_tensor(y[:], acc[:], tt[half, pair][:], MULT)
-                ys.append(y)
-            for i in range(PACK):
-                window = pages[i][:].indirect(list3[:, half * HALF // 16 : (half + 1) * HALF // 16])
-                nc.vector.tensor_tensor(window, ys[i // 2][:, i % 2, :], wgo_t[:, cols], MULT)
-                if half == 1:
-                    nc.sync.dma_start(out.rearrange("(p i) c -> p i c", i=PACK)[:, i, :], pages[i][:])
+        def pick(b, i, m0, width, tag=None):
+            x = keep.tile([P, width], F32, name="x%d%d_%d" % (b, i, m0), tag=tag or "x%d" % width, bufs=1 if tag else XB[width], align_bytes=64)
+            nc.vector.tensor_tensor(
+                x[:], h[b, i][:].indirect(list2[:, m0 // 16 : (m0 + width) // 16]), wgt_t[:, m0 : m0 + width], MULT
+            )
+            return x
 
-        make_t(0)
-        make_out(0)
+        def squash(rows, b, i, x):
+            nc.scalar.activation(rows[:, i, :], x, TANH, bias=b1_t[:, b, i : i + 1])
+
+        z_q = {}
+
+        def gain_z(b, half, rows, engine, tag):
+            grouped = new_grouped(HALF, "g_z%d%d" % (b, half), tag)
+            if engine == "v":
+                dst, src = interleave_views(grouped[:], rows)
+                g = gain_t[:, b, :].unsqueeze(1).unsqueeze(3).to_broadcast([P, HALF // 4, PACK, 4])
+                nc.vector.tensor_tensor(dst, src, g, MULT)
+            else:
+                zr = keep.tile([P, PACK, HALF], BF16, name="zr%d%d" % (b, half), tag="zr", bufs=2)
+                for i in range(PACK):
+                    nc.scalar.activation(zr[:, i, :], rows[:, i, :], COPY, scale=gain_t[:, b, i : i + 1])
+                dst, src = interleave_views(grouped[:], zr[:])
+                nc.vector.tensor_copy(dst, src)
+            return grouped
+
+        def cast_tmpl(a, half, engine, tag):
+            grouped = new_grouped(HALF, "g_tm%d%d" % (a, half), tag)
+            dst, src = interleave_views(grouped[:], tmpl_raw[a, half][:])
+            copy_on(engine, dst, src)
+            return grouped
+
+        tmpl_q, tt, ys = {}, {}, {}
+
+        def make_t(half, pair):
+            acc = psum.tile([P, 2, HALF], F32, name="t_acc%d%d" % (half, pair), tag="bank")
+            tt[half, pair] = keep.tile([P, 2, HALF], F32, name="tt%d%d" % (half, pair), align_bytes=64)
+            for s in range(2):
+                for a in range(2):
+                    mm(acc[:, s, :], w3_q[a, 2 * pair + s], tmpl_q[a, half][0][:], tmpl_q[a, half][1][:], a)
+            for s in range(2):
+                i = 2 * pair + s
+                nc.scalar.activation(tt[half, pair][:, s, :], acc[:, s, :], TANH, bias=b3_t[:, i : i + 1])
+
+        def make_y(half, pair):
+            acc = psum.tile([P, 2, HALF], F32, name="f_acc%d%d" % (half, pair), tag="bank")
+            for s in range(2):
+                i = 2 * pair + s
+                for c in range(2):
+                    part = slice(c * P, (c + 1) * P)
+                    for b in range(2):
+                        nc.tensor.matmul_mx(
+                            out=acc[:, s, part],
+                            lhsT=w4_wd[:, b, 2 * P * i : 2 * P * (i + 1)].bitcast(FP4X4),
+                            lhsT_scale=w4_sd[:, b, P * i : P * (i + 1)],
+                            rhs=z_q[b, half][0][:, part].bitcast(FP8X4),
+                            rhs_scale=z_q[b, half][1][:, part],
+                            start=(b == 0), stop=(b == 1),
+                        )
+            y = keep.tile([P, 2, HALF], F32, name="y%d%d" % (half, pair), tag="y", bufs=3)
+            nc.vector.tensor_tensor(y[:], acc[:], tt[half, pair][:], MULT)
+            ys[half, pair] = y
+
+        def put(half, pair, s):
+            i = 2 * pair + s
+            window = pages[i][:].indirect(list3[:, half * HALF // 16 : (half + 1) * HALF // 16])
+            nc.vector.tensor_tensor(window, ys[half, pair][:, s, :], wgo_t[:, half * HALF : (half + 1) * HALF], MULT)
+            if half == 1:
+                nc.sync.dma_start(out.rearrange("(p i) c -> p i c", i=PACK)[:, i, :], pages[i][:])
+
+        make_h(0, 0, "vs")
+        for i in range(1, PACK):
+            make_h(0, i, "ss")
+        quantise_weight(cast_weight("v", w1_raw[1, 0], ALL, "g_w1_10", "g0"), ALL, "w1_10", w1_q, (1, 0))
+        quantise_weight(cast_weight("v", w1_raw[1, 1], ALL, "g_w1_11", "g3"), ALL, "w1_11", w1_q, (1, 1))
+        xs = [pick(0, i, 0, M) for i in range(PACK)]
+        quantise_weight(cast_weight("s", w3_raw[0], LO, "g_w3_0l", "g1"), LO, "w3_0l", w3_q, (0,))
         for i in range(PACK):
-            squash(1, i, [1], xb[i])
-        make_z(0, 1, "s")
-        make_z(1, 1, "s")
-        make_t(1)
-        make_out(1)
+            make_h(1, i, "ss")
+        th0 = keep.tile([P, PACK, M], F32, name="th0")
+        for i in range(PACK):
+            squash(th0, 0, i, xs[i][:])
+        xa = [pick(1, i, 0, HALF)[:] for i in range(PACK)]
+        quantise_weight(cast_weight("s", w3_raw[1], LO, "g_w3_1l", "g2"), LO, "w3_1l", w3_q, (1,))
+        z_q[0, 0] = quantise(gain_z(0, 0, th0[:, :, 0:HALF], "v", "g0"), HALF, "z00")
+        th1a = keep.tile([P, PACK, HALF], F32, name="th1a")
+        for i in range(PACK):
+            squash(th1a, 1, i, xa[i])
+        z_q[1, 0] = quantise(gain_z(1, 0, th1a[:], "v", "g3"), HALF, "z10")
+        for a in range(2):
+            tmpl_q[a, 0] = quantise(cast_tmpl(a, 0, "s", "g%d" % (4 + a)), HALF, "tm%d0" % a)
+        xb = [pick(1, i, HALF, HALF, None)[:] for i in range(PACK)]
+        make_t(0, 0)
+        make_y(0, 0)
+        put(0, 0, 0)
+        z_q[0, 1] = quantise(gain_z(0, 1, th0[:, :, HALF:M], "v", "g0"), HALF, "z01")
+        for a in range(2):
+            quantise_weight(cast_weight("s", w3_raw[a], HI, "g_w3_%dh" % a, "g%d" % (1 + a)), HI, "w3_%dh" % a, w3_q, (a,))
+        for a in range(2):
+            tmpl_q[a, 1] = quantise(cast_tmpl(a, 1, "s", "g%d" % (4 + a)), HALF, "tm%d1" % a)
+        th1b = keep.tile([P, PACK, HALF], F32, name="th1b")
+        for i in range(PACK):
+            squash(th1b, 1, i, xb[i])
+        z_q[1, 1] = quantise(gain_z(1, 1, th1b[:], "s", "g3"), HALF, "z11")
+        make_t(0, 1)
+        make_y(0, 1)
+        put(0, 0, 1)
+        put(0, 1, 0)
+        make_t(1, 0)
+        make_y(1, 0)
+        put(0, 1, 1)
+        put(1, 0, 0)
+        make_t(1, 1)
+        make_y(1, 1)
+        put(1, 0, 1)
+        put(1, 1, 0)
+        put(1, 1, 1)

from contextlib import ExitStack

import concourse.mybir as mybir

K, H, N, T, S, M, T2 = 1024, 1024, 512, 4096, 1024, 512, 1024
FLOPS = 2 * (K * H * S + H * N * M + K * N * M)

F32 = mybir.dt.float32
BF16 = mybir.dt.bfloat16
I32 = mybir.dt.int32
U32 = mybir.dt.uint32
U16 = mybir.dt.uint16
U8 = mybir.dt.uint8
FP8X4 = mybir.dt.float8_e4m3fn_x4
FP4X4 = mybir.dt.float4_e2m1fn_x4
MULT = mybir.AluOpType.mult
TANH = mybir.ActivationFunctionType.Tanh
COPY = mybir.ActivationFunctionType.Copy

P = 128
PACK = 4
KP = P * PACK
HALF = M // 2
XB = {256: 4, 512: 4}


def tile_list_braille_fault_scores_kernel(
    tc, tab_words, tab_scales, offs, w1, offs2, wgt, b1, gain, w4_words, w4_scales, tmpl, w3, b3, offs3, wgo, out
):
    nc = tc.nc
    with ExitStack() as ctx:
        keep = ctx.enter_context(tc.tile_pool(name="keep", bufs=1))
        psum = ctx.enter_context(tc.psum_pool(name="psum", bufs=8))

        list1 = keep.tile([P, S // 16], U16, name="list1")
        list2 = keep.tile([P, M // 16], U16, name="list2")
        list3 = keep.tile([P, M // 16], U16, name="list3")
        tab_w = [keep.tile([P, T], U32, name="tab_w%d" % a) for a in range(2)]
        tab_s = keep.tile([P, T], U8, name="tab_s", tag="w1_00_codes", align_bytes=64)
        w4_w = keep.tile([P, 2, 2 * N], U8, name="w4_w")
        w4_s = keep.tile([P, 2, N], U8, name="w4_s")
        wgt_t = keep.tile([P, M], F32, name="wgt_t")
        wgo_t = keep.tile([P, M], F32, name="wgo_t")
        b1_t = keep.tile([P, 2, PACK], F32, name="b1_t")
        gain_t = keep.tile([P, 2, PACK], F32, name="gain_t")
        b3_t = keep.tile([P, PACK], F32, name="b3_t")
        pages = [keep.tile([P, T2], F32, name="page%d" % i) for i in range(PACK)]
        warm_in = keep.tile([P, 1], F32, name="warm_in")
        warm_out = keep.tile([P, 1], F32, name="warm_out")

        nc.vector.memset(tab_s[:].bitcast(I32), 0)
        nc.vector.memset(warm_in[:], 0.0)
        nc.gpsimd.memset(w4_s[:].rearrange("p a c -> p (a c)").bitcast(I32), 0)
        for page in pages:
            nc.vector.memset(page[:], 0.0)

        def load_rows(src, a, c0, width, name, tag):
            raw = keep.tile([P, PACK, width], F32, name=name, tag=tag, align_bytes=64)
            rows = src[a * KP : (a + 1) * KP, c0 : c0 + width]
            nc.sync.dma_start(raw[:], rows.rearrange("(p j) c -> p j c", j=PACK))
            return raw

        def load_table(a, cols):
            words = tab_words[a].rearrange("p t i -> p (t i)").bitcast(I32)
            nc.sync.dma_start(tab_w[a][:].bitcast(I32)[:, cols], words[:, cols])

        w1_raw = {}
        nc.sync.dma_start(list1[:], offs)
        nc.scalar.activation(warm_out[:], warm_in[:], TANH)
        nc.sync.dma_start(w4_w[:].bitcast(I32), w4_words.rearrange("a p c -> p a c").bitcast(I32))
        for q in range(4):
            nc.sync.dma_start(
                w4_s[32 * q : 32 * q + 4, :, :].bitcast(I32),
                w4_scales[:, 4 * q : 4 * q + 4, :].rearrange("a r c -> r a c").bitcast(I32),
            )
        load_table(0, slice(0, T // 2))
        load_table(0, slice(T // 2, T))
        for n in range(8):
            a, q = divmod(n, 4)
            if n == 6:
                w1_raw[0, 0] = load_rows(w1, 0, 0, KP, "w1_00", "raw0")
            row = 32 * q + 4 * a
            nc.sync.dma_start(tab_s[row : row + 4, :].bitcast(I32), tab_scales[a, 4 * q : 4 * q + 4, :].bitcast(I32))
        load_table(1, slice(0, T))
        w1_raw[0, 1] = load_rows(w1, 1, 0, KP, "w1_01", "raw1")
        nc.sync.dma_start(list2[:], offs2)
        nc.sync.dma_start(wgt_t[:], wgt)
        nc.sync.dma_start(b1_t[:], b1.rearrange("(b p i) -> p b i", b=2, i=PACK))
        for a in range(2):
            w1_raw[1, a] = load_rows(w1, a, KP, KP, "w1_1%d" % a, "raw%d" % (2 + a))
        w3_raw = [load_rows(w3, a, 0, KP, "w3_%d" % a, "raw%d" % (4 + a)) for a in range(2)]
        nc.sync.dma_start(gain_t[:], gain.rearrange("(b p i) -> p b i", b=2, i=PACK))
        tmpl_raw = {}
        for a in range(2):
            tmpl_raw[a, 0] = load_rows(tmpl, a, 0, HALF, "tmpl_%d0" % a, "tma%d" % a)
        nc.sync.dma_start(list3[:], offs3)
        nc.sync.dma_start(b3_t[:], b3.rearrange("(p i) -> p i", i=PACK))
        nc.sync.dma_start(wgo_t[:], wgo)
        for a in range(2):
            tmpl_raw[a, 1] = load_rows(tmpl, a, HALF, HALF, "tmpl_%d1" % a, "raw%d" % (2 + a))

        def copy_on(engine, dst, src):
            if engine == "v":
                nc.vector.tensor_copy(dst, src)
            else:
                nc.scalar.copy(dst, src)

        def quantise(grouped, width, name):
            codes = keep.tile([P, width], U32, name=name + "_codes", align_bytes=64)
            scales = keep.tile([P, width], U8, name=name + "_scales", align_bytes=64)
            nc.vector.quantize_mx(out=codes[:].bitcast(FP8X4), scales=scales[:], in_=grouped[:])
            return codes, scales

        def new_grouped(width, name, tag):
            return keep.tile([P, width * PACK], BF16, name=name, tag=tag, align_bytes=64)

        def cast_weight(engine, raw, slots, name, tag):
            grouped = new_grouped(P * len(slots), name, tag)
            copy_on(
                engine,
                grouped[:].rearrange("p (t q j) -> p q j t", t=len(slots), j=PACK),
                raw[:].rearrange("p j (q t) -> p q j t", t=PACK)[:, :, :, slots[0] : slots[-1] + 1],
            )
            return grouped

        def quantise_weight(grouped, slots, name, into, key):
            codes, scales = quantise(grouped, P * len(slots), name)
            for n, slot in enumerate(slots):
                into[key + (slot,)] = (codes[:, n * P : (n + 1) * P], scales[:, n * P : (n + 1) * P])

        def interleave_views(grouped, rows):
            return (
                grouped.rearrange("p (c u j) -> p c j u", u=4, j=PACK),
                rows.rearrange("p j (c u) -> p c j u", u=4),
            )

        def mm(acc, lhs, rhs_codes, rhs_scales, a):
            nc.tensor.matmul_mx(
                out=acc, lhsT=lhs[0].bitcast(FP8X4), lhsT_scale=lhs[1],
                rhs=rhs_codes.bitcast(FP8X4), rhs_scale=rhs_scales, start=(a == 0), stop=(a == 1),
            )

        w4_wd = keep.tile([P, 2, 2 * N], U8, name="w4_wd", align_bytes=64)
        w4_sd = keep.tile([P, 2, N], U8, name="w4_sd", align_bytes=64)
        nc.vector.tensor_copy(
            w4_wd[:].bitcast(U16).rearrange("p a (t q) -> p a q t", t=PACK),
            w4_w[:].bitcast(U16).rearrange("p a (q t) -> p a q t", t=PACK),
        )
        nc.vector.tensor_copy(
            w4_sd[:].rearrange("p a (t q) -> p a q t", t=PACK), w4_s[:].rearrange("p a (q t) -> p a q t", t=PACK)
        )

        v_s = keep.tile([P, S], U8, name="v_s", align_bytes=64)
        v_w = [keep.tile([P, S], U32, name="v_w0", align_bytes=64)]
        nc.vector.tensor_copy(v_w[0][:], tab_w[0][:].indirect(list1[:]))
        nc.vector.tensor_copy(v_s[:], tab_s[:].indirect(list1[:]))
        w1_q, w3_q = {}, {}
        ALL, LO, HI = [0, 1, 2, 3], [0, 1], [2, 3]
        quantise_weight(cast_weight("s", w1_raw[0, 0], ALL, "g_w1_00", "vw1"), ALL, "w1_00", w1_q, (0, 0))
        v_w.append(keep.tile([P, S], U32, name="v_w1", tag="vw1", align_bytes=64))
        nc.vector.tensor_copy(v_w[1][:], tab_w[1][:].indirect(list1[:]))
        lo = cast_weight("v", w1_raw[0, 1], LO, "g_w1_01l", "g1")
        hi = cast_weight("s", w1_raw[0, 1], HI, "g_w1_01h", "g2")
        quantise_weight(lo, LO, "w1_01l", w1_q, (0, 1))
        quantise_weight(hi, HI, "w1_01h", w1_q, (0, 1))

        h = {}

        def make_h(b, i, engines):
            h[b, i] = keep.tile([P, S], F32, name="h%d%d" % (b, i), tag="h", bufs=5)
            for c in range(2):
                cols = slice(c * KP, (c + 1) * KP)
                acc = psum.tile([P, KP], F32, name="h_acc%d%d%d" % (b, i, c), tag="bank")
                for a in range(2):
                    mm(acc[:], w1_q[b, a, i], v_w[a][:, cols], v_s[4 * a : P, cols], a)
                copy_on(engines[c], h[b, i][:, cols], acc[:])

        def pick(b, i, m0, width, tag=None):
            x = keep.tile([P, width], F32, name="x%d%d_%d" % (b, i, m0), tag=tag or "x%d" % width, bufs=1 if tag else XB[width], align_bytes=64)
            nc.vector.tensor_tensor(
                x[:], h[b, i][:].indirect(list2[:, m0 // 16 : (m0 + width) // 16]), wgt_t[:, m0 : m0 + width], MULT
            )
            return x

        def squash(rows, b, i, x):
            nc.scalar.activation(rows[:, i, :], x, TANH, bias=b1_t[:, b, i : i + 1])

        z_q = {}

        def gain_z(b, half, rows, engine, tag):
            grouped = new_grouped(HALF, "g_z%d%d" % (b, half), tag)
            if engine == "v":
                dst, src = interleave_views(grouped[:], rows)
                g = gain_t[:, b, :].unsqueeze(1).unsqueeze(3).to_broadcast([P, HALF // 4, PACK, 4])
                nc.vector.tensor_tensor(dst, src, g, MULT)
            else:
                zr = keep.tile([P, PACK, HALF], BF16, name="zr%d%d" % (b, half), tag="zr", bufs=2)
                for i in range(PACK):
                    nc.scalar.activation(zr[:, i, :], rows[:, i, :], COPY, scale=gain_t[:, b, i : i + 1])
                dst, src = interleave_views(grouped[:], zr[:])
                nc.vector.tensor_copy(dst, src)
            return grouped

        def cast_tmpl(a, half, engine, tag):
            grouped = new_grouped(HALF, "g_tm%d%d" % (a, half), tag)
            dst, src = interleave_views(grouped[:], tmpl_raw[a, half][:])
            copy_on(engine, dst, src)
            return grouped

        tmpl_q, tt, ys = {}, {}, {}

        def make_t(half, pair):
            acc = psum.tile([P, 2, HALF], F32, name="t_acc%d%d" % (half, pair), tag="bank")
            tt[half, pair] = keep.tile([P, 2, HALF], F32, name="tt%d%d" % (half, pair), align_bytes=64)
            for s in range(2):
                for a in range(2):
                    mm(acc[:, s, :], w3_q[a, 2 * pair + s], tmpl_q[a, half][0][:], tmpl_q[a, half][1][:], a)
            for s in range(2):
                i = 2 * pair + s
                nc.scalar.activation(tt[half, pair][:, s, :], acc[:, s, :], TANH, bias=b3_t[:, i : i + 1])

        def make_y(half, pair):
            acc = psum.tile([P, 2, HALF], F32, name="f_acc%d%d" % (half, pair), tag="bank")
            for s in range(2):
                i = 2 * pair + s
                for c in range(2):
                    part = slice(c * P, (c + 1) * P)
                    for b in range(2):
                        nc.tensor.matmul_mx(
                            out=acc[:, s, part],
                            lhsT=w4_wd[:, b, 2 * P * i : 2 * P * (i + 1)].bitcast(FP4X4),
                            lhsT_scale=w4_sd[:, b, P * i : P * (i + 1)],
                            rhs=z_q[b, half][0][:, part].bitcast(FP8X4),
                            rhs_scale=z_q[b, half][1][:, part],
                            start=(b == 0), stop=(b == 1),
                        )
            y = keep.tile([P, 2, HALF], F32, name="y%d%d" % (half, pair), tag="y", bufs=3)
            nc.vector.tensor_tensor(y[:], acc[:], tt[half, pair][:], MULT)
            ys[half, pair] = y

        def put(half, pair, s):
            i = 2 * pair + s
            window = pages[i][:].indirect(list3[:, half * HALF // 16 : (half + 1) * HALF // 16])
            nc.vector.tensor_tensor(window, ys[half, pair][:, s, :], wgo_t[:, half * HALF : (half + 1) * HALF], MULT)
            if half == 1:
                nc.sync.dma_start(out.rearrange("(p i) c -> p i c", i=PACK)[:, i, :], pages[i][:])

        make_h(0, 0, "vs")
        for i in range(1, PACK):
            make_h(0, i, "ss")
        quantise_weight(cast_weight("v", w1_raw[1, 0], ALL, "g_w1_10", "g0"), ALL, "w1_10", w1_q, (1, 0))
        quantise_weight(cast_weight("v", w1_raw[1, 1], ALL, "g_w1_11", "g3"), ALL, "w1_11", w1_q, (1, 1))
        xs = [pick(0, i, 0, M) for i in range(PACK)]
        quantise_weight(cast_weight("s", w3_raw[0], LO, "g_w3_0l", "g1"), LO, "w3_0l", w3_q, (0,))
        for i in range(PACK):
            make_h(1, i, "ss")
        th0 = keep.tile([P, PACK, M], F32, name="th0")
        for i in range(PACK):
            squash(th0, 0, i, xs[i][:])
        xa = [pick(1, i, 0, HALF)[:] for i in range(PACK)]
        quantise_weight(cast_weight("s", w3_raw[1], LO, "g_w3_1l", "g2"), LO, "w3_1l", w3_q, (1,))
        z_q[0, 0] = quantise(gain_z(0, 0, th0[:, :, 0:HALF], "v", "g0"), HALF, "z00")
        th1a = keep.tile([P, PACK, HALF], F32, name="th1a")
        for i in range(PACK):
            squash(th1a, 1, i, xa[i])
        z_q[1, 0] = quantise(gain_z(1, 0, th1a[:], "v", "g3"), HALF, "z10")
        for a in range(2):
            tmpl_q[a, 0] = quantise(cast_tmpl(a, 0, "s", "g%d" % (4 + a)), HALF, "tm%d0" % a)
        xb = [pick(1, i, HALF, HALF, None)[:] for i in range(PACK)]
        make_t(0, 0)
        make_y(0, 0)
        put(0, 0, 0)
        z_q[0, 1] = quantise(gain_z(0, 1, th0[:, :, HALF:M], "v", "g0"), HALF, "z01")
        for a in range(2):
            quantise_weight(cast_weight("s", w3_raw[a], HI, "g_w3_%dh" % a, "g%d" % (1 + a)), HI, "w3_%dh" % a, w3_q, (a,))
        for a in range(2):
            tmpl_q[a, 1] = quantise(cast_tmpl(a, 1, "s", "g%d" % (4 + a)), HALF, "tm%d1" % a)
        th1b = keep.tile([P, PACK, HALF], F32, name="th1b")
        for i in range(PACK):
            squash(th1b, 1, i, xb[i])
        z_q[1, 1] = quantise(gain_z(1, 1, th1b[:], "s", "g3"), HALF, "z11")
        make_t(0, 1)
        make_y(0, 1)
        put(0, 0, 1)
        put(0, 1, 0)
        make_t(1, 0)
        make_y(1, 0)
        put(0, 1, 1)
        put(1, 0, 0)
        make_t(1, 1)
        make_y(1, 1)
        put(1, 0, 1)
        put(1, 1, 0)
        put(1, 1, 1)
